import numpy as np, ml_dtypes
CORES = [3,11,19,27,35,43,51,59]
N = 8
BF = ml_dtypes.bfloat16
V, M, E, RO, LINKS = 2048, 1024, 320, 3, 8
GR = np.arange(8)
def pairs(s):
    o = np.argsort(-s, axis=2, kind="stable")
    b = np.stack([np.sum(s > 15 - c, axis=2) for c in range(16)], 2) >> 1
    e = np.concatenate([b[:, :, 1:], np.full_like(b[:, :, :1], M)], 2)
    t = np.arange(M); j = np.sum(b[:, :, :, None] <= t, axis=2) - 1
    bt = np.take_along_axis(b, j, 2); h = np.take_along_axis(e, j, 2) - bt
    return np.take_along_axis(o, bt + t, 2), np.take_along_axis(o, bt + t + h, 2), t - bt, h
def pick(a, ix):
    return np.take_along_axis(a, ix[:, :, None, :], 3)
def swap(a):
    z = a.copy()
    for r in range(LINKS):
        q = (r + 1) % N
        z[r, ..., V - E:] = a[q, ..., :E]; z[q, ..., :E] = a[r, ..., V - E:]
    return z
def pool(rng, m):
    return np.stack([rng.choice(2 ** 20 - 1, m, replace=False) + 1 for g in range(8)])
def boards(rng):
    close = rng.choice(np.array([0, 60, 99, 100, 101, 190]), (N, 8, 1, V)) + (rng.random((N, 8, 16, V)) * rng.choice(np.array([1, 3, 8, 11]), (N, 8, 1, V))).astype(np.int64)
    return np.where(rng.random((N, 8, 1, V)) < 0.4, rng.integers(0, 201, (N, 8, 16, V)), close)
def scores(rng):
    w = rng.choice(np.array([0.5, 1.0, 2.0]), (N, 8, 1))
    return np.minimum((4 * rng.random((N, 8, V)) ** w).astype(np.int64), 3)
def clubs(rng, m):
    a = pool(rng, int(np.max(m)))
    n = a[GR[:, None], (rng.random((N, 8, V)) * m[:, None]).astype(np.int64)]
    p = a[GR[:, None, None], (rng.random((N, 8, 16, V)) * m[:, None, None]).astype(np.int64)]
    return n, np.where(np.arange(16)[:, None] < rng.integers(0, 25, (N, 8, 1, V)), p, 0)
def plant(rng, p, who, name, mask):
    w = np.ascontiguousarray(p).reshape(N, 8, 16 * V); ix = rng.integers(0, 16, who.shape) * V + who
    np.put_along_axis(w, ix, np.where(mask, name, np.take_along_axis(w, ix, 2)), 2)
    return w.reshape(N, 8, 16, V)
def pack(v, p, n, s):
    return {"x": np.ascontiguousarray(v.reshape(N, 128, V)).astype(np.float32).astype(BF), "hi": np.ascontiguousarray(p.reshape(N, 128, V)).astype(np.int32),
            "nm": np.ascontiguousarray(n).astype(np.int32), "sc": np.ascontiguousarray(s).astype(np.int32)}
def setup_inputs(rng):
    n, p = clubs(rng, rng.permutation(np.array([40, 80, 120, 160, 240, 320, 480, 640])))
    return pack(boards(rng), p, n, scores(rng))
def setup_inputs_ends(rng):
    q = V // 4
    cs = [(V, 0, 0, 0), (0, 0, V, 0), (1, 1, 1, V - 3), (V - 3, 1, 1, 1), (0, 1, V - 2, 1), (1, 0, V - 1, 0), (2, 0, V - 5, 3), (q + 1, q - 1, q + 1, q - 1),
          (0, 0, 0, V), (q + 1, 0, 0, V - q - 1), (0, V, 0, 0), (1, 0, 0, V - 1), (0, 0, 1, V - 1), (1, V - 2, 0, 1), (0, q - 1, 0, V - q + 1), (V - 3, 0, 0, 3)]
    s = np.zeros((N, 8, V), np.int64)
    for r in range(N):
        o = rng.permutation(16)[:8] if r > 1 else 8 * r + np.arange(8)
        for g in range(8): s[r, g] = rng.permutation(np.repeat(np.array([3, 2, 1, 0]), cs[int(o[g])]))
    n, p = clubs(rng, rng.permutation(np.array([40, 80, 120, 160, 240, 320, 480, 640])))
    return pack(boards(rng), p, n, s)
def setup_inputs_met(rng):
    s = scores(rng); a = pool(rng, N * V); n = np.ascontiguousarray(a.reshape(8, N, V).transpose(1, 0, 2))
    s[:2, 7] = rng.integers(0, 4, (2, 1))
    for r in (2, 3): s[r, 6] = rng.permutation(np.repeat(np.array([3, 2, 1, 0]), (4, 4, 4, V - 12)))
    p = a[GR[:, None, None], rng.integers(0, N * V, (N, 8, 16, V))]
    U, L, i, h = pairs(s); nu, nl = np.take_along_axis(n, U, 2), np.take_along_axis(n, L, 2)
    for r in (2, 3): p[r, 6][:, U[r, 6, 0:6:2]] = 0
    share = rng.choice(np.array([0.0, 0.02, 0.1, 0.3, 0.5, 0.9, 1.0]), (N, 8, 1)); share[0, :, 0] = (0.0, 0.02, 0.1, 0.3, 0.5, 0.7, 0.9, 1.0); share[1, 7] = 1.0
    again = (rng.random((N, 8, M)) < share) | ((i == h - 1) & (h % 2 == 1)); again[2:4, 6, :6] = np.arange(6) % 2 == 1
    p = plant(rng, p, L, nu, rng.random((N, 8, M)) < 0.3)
    p = plant(rng, p, U, np.roll(nl, -1, 2), rng.random((N, 8, M)) < 0.1)
    p = plant(rng, p, U, nl, again)
    return pack(boards(rng), p, n, s)
def setup_inputs_ties(rng):
    v = boards(rng); kind = rng.integers(0, 2, (N, 1, V)); row = np.arange(16)[:, None]
    v[:, 0] = 100
    v[:, 1] = np.where((row < 8) == (kind == 1), 150, 50)
    v[:, 2] = 200 * rng.integers(0, 2, (N, 16, V))
    v[:, 3] = 100 + (row == rng.integers(0, 16, (N, 1, V)))
    v[:, 4] = 100 + rng.integers(0, 2, (N, 16, V))
    v[:, 5] = np.where(kind == 1, 200, 0)
    n, p = clubs(rng, rng.permutation(np.array([40, 80, 120, 160, 240, 320, 480, 640])))
    s = scores(rng); s[:, 0] = np.where(np.arange(N)[:, None] % 2 == 0, rng.integers(0, 4, (N, 1)), s[:, 0])
    return pack(v, p, n, s)
def setup_inputs_alike(rng):
    n, p = clubs(rng, np.array([1, 1, 2, 3, 5, 17, 17, 400]))
    p[:, 1] = 0; p[:, 3] = 0; p[:, 5] = p[:, 5, :1].copy(); p[:, 6, :15] = 0
    n[:, 2] = np.where(rng.random((N, V)) < 0.5, 1, 2 ** 20 - 1); p[:, 2] = rng.choice(np.array([0, 1, 2 ** 20 - 1]), (N, 16, V))
    n[:, 3] = rng.integers(1, 4, (N, V))
    n[:, 7] = 2 ** 20 - 1 - rng.integers(0, 3, (N, V)); p[:, 7] = rng.integers(0, 3, (N, 16, V))
    return pack(boards(rng), p, n, scores(rng))
def setup_inputs_spread(rng):
    v = np.minimum((np.exp2(8 * rng.random((N, 8, 1, V))) * rng.random((N, 8, 16, V))).astype(np.int64), 200)
    n = np.minimum(np.exp2(20 * rng.random((N, 8, V))).astype(np.int64), 2 ** 20 - 1)
    p = np.minimum(np.exp2(20 * rng.random((N, 8, 16, V))).astype(np.int64), 2 ** 20 - 1) * (rng.random((N, 8, 16, V)) > 0.0625)
    n[:, 7] = 2 ** 20 - 1 - rng.integers(0, 200, (N, V)); p[:, 7] = 2 ** 20 - 1 - rng.integers(0, 200, (N, 16, V))
    return pack(v, p, n, np.minimum((4 * rng.random((N, 8, V)) ** 4).astype(np.int64), 3))
def check_inputs(d):
    bad = []
    for k, lo, hi_ in (("x", 0, 200), ("hi", 0, 2 ** 20 - 1), ("nm", 1, 2 ** 20 - 1), ("sc", 0, 3)):
        a = np.asarray(d[k]).astype(np.float64)
        if not np.all((a >= lo) & (a <= hi_)): bad.append("range of " + k)
        elif not np.all(a == np.floor(a)): bad.append("whole numbers in " + k)
    return bad
def reference(x, hi, nm, sc):
    v = x.astype(np.float32).astype(np.int32).reshape(N, 8, 16, V); p = hi.astype(np.int32).reshape(N, 8, 16, V)
    n = nm.astype(np.int32); s = sc.astype(np.int32)
    for rnd in range(RO):
        U, L, i, h = pairs(s)
        pu = pick(p, U)
        met = np.any(pu == np.take_along_axis(n, L, 2)[:, :, None, :], axis=2)
        ex = ((i & 1) == 0) & (i + 1 < h) & (met | np.roll(met, -1, 2))
        L = np.where(ex, np.roll(L, -1, 2), np.where(np.roll(ex, 1, 2), np.roll(L, 1, 2), L))
        xu, xl, pl = pick(v, U), pick(v, L), pick(p, L)
        nu, nl = np.take_along_axis(n, U, 2), np.take_along_axis(n, L, 2)
        wu, wl = np.sum(xu > xl, axis=2), np.sum(xl > xu, axis=2)
        su = np.take_along_axis(s, U, 2) + 2 * (wu > wl) + (wu == wl); sl = np.take_along_axis(s, L, 2) + 2 * (wl > wu) + (wu == wl)
        v = swap(np.concatenate([xu + (xl > xu), xl + (xu > xl)], 3))
        p = swap(np.concatenate([np.concatenate([nl[:, :, None, :], pu[:, :, :15]], 2), np.concatenate([nu[:, :, None, :], pl[:, :, :15]], 2)], 3))
        n = swap(np.concatenate([nu, nl], 2)); s = swap(np.concatenate([su, sl], 2))
    return {"yx": v.reshape(N, 128, V).astype(np.float32).astype(BF), "yn": n.astype(np.float32), "ys": s.astype(np.float32)}

from concourse.bass import DstId, RemoteDMATransfer
from concourse.mybir import AluOpType as ALU, ActivationFunctionType as ACT

V, M, E, RO = 2048, 1024, 320, 3
WB = V + 2 * E
S_INT = True
MAGIC = 12582912.0

SCRATCH = {}


def _sb(names, cols, dtype):
    for n in names.split():
        SCRATCH[n] = ("sbuf", [128, cols], dtype)


_sb("X0 X1 X2 X3 M0 M1 M2 M3", WB, "bfloat16")
_sb("H0", WB, "int32")
_sb("H1 H2", WB, "float32")
_sb("H3", M, "float32")
_sb("W C IP", V, "bfloat16")
_sb("ML XU DD SS RR EQ OH RS", M, "bfloat16")
_sb("AA AB AC JJ", M, "float16")
_sb("sc0 sc1 sc2", 144, "bfloat16")
_sb("sci nmi", 128, "int32")
_sb("nmp", 384, "int32")
_sb("PC", 640, "bfloat16")
_sb("LT", E, "bfloat16")
_sb("scb sct mask mOE", 128, "bfloat16")
_sb("TI i16 y2 LOE", 128, "float16")
_sb("y1 DI F0 LS fo fn basef", 128, "float32")
_sb("off", 128, "uint16")
_sb("lu ll", 64, "uint16")
_sb("sig", 64, "float32")
_sb("st0 st1", 48, "bfloat16")
_sb("stf lf", 80, "float32")
_sb("eb eb2", 16, "float32")
_sb("nb1 nb2 t1 d1 e2 sb hh", 8, "float32")
_sb("cm", 8, "bfloat16")
_sb("pi pj", 4, "int32")
_sb("col lt ge th", 24, "float32")
_sb("TT TR", 320, "float32")
_sb("iw gm zu", 160, "float32")
_sb("Iw Z1 Zp Zn", 160, "bfloat16")
_sb("B Hb nB Tq Tp nI Y00 Y11 Y01 Y10 Nb Ob1 Ob2 Iz0 Iz1 Sh0 Sh1 Sup Sdn Wup Wdn", 128, "bfloat16")
PS = "P0 P1 N0 N1 N2 Q0 Q1 Q2".split()
for _n in PS:
    SCRATCH[_n] = ("psum", [128, 512], "float32")

NDMA = 40
SEMAPHORES = ["cv", "cs", "ct", "cg", "sent"] + ["d%d" % i for i in range(NDMA)] + \
             ["%s%d" % (n, k) for n in ("rs", "rm", "rx", "rh") for k in range(RO)]


def _meets(a, b):
    return a[0] == b[0] and (a[0] in PS or (a[1] < b[2] and b[1] < a[2]))


def _emit(g, T, ops):
    eng = {"v": g.vector, "s": g.scalar, "t": g.tensor, "g": g, "y": g.sync}
    known = {q: {} for q in eng}
    clock, waits, needed = [], [], set()
    by_buf = {}
    for i, o in enumerate(ops):
        q, deps = o["q"], set()
        regs = [(r, False) for r in o["r"]] + [(r, True) for r in o["w"]]
        for reg, wr in regs:
            for j, reg2, wr2 in by_buf.get(reg[0], []):
                if not _meets(reg, reg2):
                    continue
                p = ops[j]
                if p["q"] == q and p["kind"] == "c" and o["kind"] == "c":
                    if wr2 and not wr and reg[1] < reg2[2] and reg2[1] < reg[2]:
                        deps.add(j)
                elif wr or wr2 or reg[0] in PS:
                    deps.add(j)
        for reg, wr in regs:
            by_buf.setdefault(reg[0], []).append((i, reg, wr))
        mine = []
        if q is not None:
            for j in sorted(deps, reverse=True):
                src = ops[j]["q"] if ops[j]["kind"] == "c" else j
                if known[q].get(src, -1) >= j:
                    continue
                mine.append(j)
                needed.add(j)
                known[q][src] = j
                for s2, v2 in clock[j].items():
                    if known[q].get(s2, -1) < v2:
                        known[q][s2] = v2
        waits.append(mine)
        clock.append(dict(known[q]) if q is not None else {})
    count = {q: 0 for q in eng}
    token, ndma, sent = {}, 0, 0
    for i, o in enumerate(ops):
        q = o["q"]
        if o["kind"] == "a":
            token[i] = (o["sem"], o["n"])
            continue
        for j in waits[i]:
            eng[q].wait_ge(T.sem[token[j][0]], token[j][1])
        ins = o["f"](eng[q])
        if o["kind"] == "c" and i in needed:
            count[q] += 1
            token[i] = ("c" + q, count[q])
            ins.then_inc(T.sem["c" + q], 1)
        elif o["kind"] == "d":
            token[i] = ("d%d" % ndma, 16)
            ins.then_inc(T.sem["d%d" % ndma], 16)
            ndma += 1
        elif o["kind"] == "r":
            sent += o["n"]
    for i, o in enumerate(ops):
        if o["kind"] == "d" and i not in needed:
            g.sync.wait_ge(T.sem[token[i][0]], 16)
    g.wait_ge(T.sem.sent, sent)


def rank_program(g, core, T, topo):
    rank = T.rank_of(core)
    if rank is None:
        return
    n = len(T.cores)
    prv, nxt = T.cores[(rank - 1) % n], T.cores[(rank + 1) % n]
    ops = []

    def A(name, a, b, step=1):
        return (T[name][:, a:b:step] if step > 1 else T[name][:, a:b], (name, a, b))

    def IND(name, a, b, off, c, d):
        return (T[name][:, a:b].indirect(T[off][:, c:d]), (name, a, b), (off, c, d))

    def col(i):
        return A("col", i, i + 1)

    def op(q, f, outs, ins, kind="c", **kw):
        r, w = [], []
        for x in outs:
            w.append(x[1])
            r.extend(x[2:])
        for x in ins:
            if isinstance(x, tuple):
                r.extend(x[1:])
        ops.append(dict(q=q, f=f, r=r, w=w, kind=kind, **kw))

    def val(x):
        return x[0] if isinstance(x, tuple) else x

    def ts(out, a, s1, o0, s2=None, o1=None):
        if o1 is None:
            op("v", lambda e: e.tensor_scalar(out[0], a[0], val(s1), None, o0), [out], [a, s1])
        else:
            op("v", lambda e: e.tensor_scalar(out[0], a[0], val(s1), val(s2), o0, o1), [out], [a, s1, s2])

    def tt(out, a, b, o):
        op("v", lambda e: e.tensor_tensor(out[0], a[0], b[0], o), [out], [a, b])

    def cp(out, a):
        op("v", lambda e: e.tensor_copy(out[0], a[0]), [out], [a])

    def ms(out, c):
        op("v", lambda e: e.memset(out[0], c), [out], [])

    def scan(out, a, b, init, o0, o1):
        op("v", lambda e: e.tensor_tensor_scan(out[0], a[0], b[0], init, o0, o1), [out], [a, b])

    def act(out, a, func=ACT.Identity, bias=0.0, scale=1.0):
        op("s", lambda e: e.activation(out[0], a[0], func, bias=val(bias), scale=val(scale)), [out], [a, bias, scale])

    def mm(terms, start=True, stop=True):
        for i, (out, l, r) in enumerate(terms):
            op("t", lambda e, out=out, l=l, r=r, i=i: e.matmul(out[0], l[0], r[0], start and i == 0,
                                                               stop and i == len(terms) - 1), [out], [l, r])

    def iota(out, pat, base, cm, flt=True):
        if flt:
            op("g", lambda e: e.iota(out[0], pat, base, cm, allow_small_or_imprecise_dtypes=True), [out], [])
        else:
            op("g", lambda e: e.iota(out[0], pat, base, cm), [out], [])

    def dma(q, out, in_):
        op(q, lambda e: e.dma_start(out[0], in_[0]), [out], [in_], kind="d")

    def hbm(ap, name, a=0, b=V):
        return (ap, ("hbm_" + name, a, b))

    ep, en = topo.engines(core, prv), topo.engines(core, nxt)
    h1 = ep[:len(ep) // 2]
    h2 = [x for x in en if x not in h1][:len(h1)]

    def bits(l):
        return sum(1 << x for x in l)

    def send1(dst, engs, src, land, sem):
        rid, pid, _ = topo.addr(dst)
        op("g", lambda e: e.remote_dma(land[0], src[0], T.sem[sem], T.sem.sent, pid, rid, bits(engs)), [], [src],
           kind="r", n=len(engs))

    def send2(src_p, land_p, src_n, land_n, sem):
        def f(e):
            tr = []
            for dst, engs, s, l in ((prv, h1, src_p, land_p), (nxt, h2, src_n, land_n)):
                rid, pid, _ = topo.addr(dst)
                tr.append(RemoteDMATransfer(dst_ids=[DstId(rid=rid, pnc=pid)], dma_engine_mask=bits(engs),
                                            remote_sem=T.sem[sem], src=s[0], dst=l[0]))
            return e.remote_dma_fused(tr, local_sem=T.sem.sent)
        op("g", f, [], [src_p, src_n], kind="r", n=len(h1) + len(h2))

    def arrive(sem, cnt, *regs):
        op(None, None, list(regs), [], kind="a", sem=sem, n=cnt)

    n_half = len(topo.engines(nxt, core)) // 2 + len(topo.engines(prv, core)) // 2
    n_full = len(topo.engines(nxt, core)) + len(topo.engines(prv, core))

    def mat(name):
        return A(name, 0, 128)

    def band(z, j):
        return A(z, 15 - j, 143 - j)

    def shift(s):
        return A("Iw", 16 - s, 144 - s)

    I = shift(0)
    G16, R, B4, NB4, O1, O2, R2, R40, R48, R128, NG = range(11)

    def lt(j):
        return A("lt", j, j + 1)

    def ge(j):
        return A("ge", j, j + 1)

    dma("y", A("sci", 0, 128), hbm(T.sc[:], "sc"))
    dma("s", A("nmi", 0, 128), hbm(T.nm[:], "nm"))
    iota(A("pi", 0, 1), [[0, 1]], 0, 1, False)
    iota(A("iw", 0, 160), [[1, 160]], -16, -1)
    iota(A("gm", 0, 128), [[16, 8], [0, 16]], 0, 0)
    iota(A("th", 0, 18), [[1, 18]], 0, 0)
    iota(A("PC", 384, 512), [[1, 128]], 0, 0)
    ms(A("cm", 0, 8), -1.0 / 32)
    ms(A("eb", 0, 1), 0.0)
    ms(A("eb2", 0, 1), 1024.0)
    for i, b in enumerate((112, 15, 16)):
        ts(A("pj", i, i + 1), A("pi", 0, 1), b, ALU.bitwise_and)
    cp(A("col", 0, 3), A("pj", 0, 3))
    ts(col(NB4), col(B4), 0.0, ALU.is_equal)
    ts(col(B4), col(B4), 1.0, ALU.min)
    ts(A("Iw", 0, 160), A("iw", 0, 160), 0.0, ALU.is_equal)
    ms(A("M0", 0, M), 0.0)
    ts(mat("B"), A("gm", 0, 128), col(G16), ALU.is_equal)
    ts(A("lt", 0, 18), A("th", 0, 18), col(R), ALU.is_gt)
    ts(A("ge", 0, 18), A("th", 0, 18), col(R), ALU.is_le)
    ms(A("M0", M, V), 0.0)
    act(col(R128), col(R), scale=128.0)
    act(mat("Y00"), I, scale=col(NB4))
    act(mat("Y01"), shift(16), scale=col(NB4))
    act(mat("Y11"), I, scale=col(B4))
    act(mat("Y10"), shift(-16), scale=col(B4))
    act(mat("nB"), mat("B"), scale=-1.0)
    act(A("PC", 512, 640), A("PC", 384, 512), bias=col(R128), scale=0.0)
    act(mat("Hb"), mat("B"), scale=0.5)
    act(mat("nI"), I, scale=-1.0)
    op("g", lambda e: e.affine_select(T.Tq[:, 0:128], T.nB[:, 0:128], [[-1, 128]], ALU.is_gt, 0.0, 0, 1),
       [mat("Tq")], [mat("nB")])
    op("g", lambda e: e.affine_select(T.Tp[:, 0:128], T.Tq[:, 0:128], [[-1, 128]], ALU.not_equal, 4096.0, 0, 1),
       [mat("Tp")], [mat("Tq")])
    iota(A("zu", 0, 160), [[1, 160]], -15, 0)
    iota(A("TR", 0, 128), [[1, 2], [32, 64]], 0, 0)
    iota(A("TR", 128, 192), [[32, 64]], 3, 0)
    iota(A("TR", 192, 320), [[1, 2], [2, 64]], 0, 0)
    iota(A("C", 0, V), [[0, V]], 0, 0)

    def row_dma(buf, row, i):
        dma("y", (T[buf][row::16, 0:V], (buf + "r%d" % row, 0, 1)), A("PC", 128 * i, 128 * i + 128))
        ops[-1]["r"].append((buf, 0, V))
        return (None, (buf + "r%d" % row, 0, 1))

    rows0 = [row_dma("M0", 14, 3), row_dma("M0", 15, 4)]
    cp(mat("scb"), mat("sci"))
    op("v", lambda e: e.transpose(T.sct[:, 0:128], T.scb[:, 0:128]), [mat("sct")], [mat("scb")])
    for i, b in enumerate((0xFF, 0xFF00, 0xF0000)):
        ts(A("nmp", 128 * i, 128 * i + 128), mat("nmi"), b, ALU.bitwise_and)
    for bb in range(4):
        for al in range(2):
            mm([(A("Q1", 2 * bb + al, 128, 8), mat("Y%d%d" % (al, ga)), A("sct", 32 * bb + 16 * ga, 32 * bb + 16 * ga + 16))
                for ga in range(2)])
    cp(A("PC", 0, 384), A("nmp", 0, 384))
    cp(A("sc0", 4, 132), A("Q1", 0, 128))
    rows0 += [row_dma("M0", i, i) for i in range(3)]
    dma("y", A("H0", 0, V), hbm(T.hi[:], "hi"))
    dma("y", A("X0", 0, V), hbm(T.x[:], "x"))
    rowsc = [row_dma("C", 14, 3), row_dma("C", 15, 4)]
    act(col(R2), col(R), scale=2.0)
    act(col(NG), col(G16), scale=-1.0)
    act(col(O1), lt(9), bias=lt(3), scale=-1.0)
    act(col(R40), col(R), scale=40.0)
    act(col(R48), col(R), scale=48.0)
    act(col(O2), ge(6), bias=col(NG))
    act(mat("F0"), A("iw", 0, 128), scale=0.0)
    for name, src, c in (("Nb", mat("B"), lt(3)), ("Sup", shift(-1), ge(1)), ("Sdn", shift(1), lt(15)),
                         ("Wup", shift(15), lt(1)), ("Wdn", shift(-15), ge(15)), ("Iz0", I, lt(3)), ("Sh0", shift(3), lt(3)),
                         ("Iz1", I, lt(14)), ("Sh1", shift(6), lt(3))):
        act(mat(name), src, scale=c)

    def late_matrices():
        act(A("gm", 0, 160), A("zu", 0, 160), ACT.Abs, bias=col(NG))
        act(A("TT", 0, 192), A("TR", 0, 192), bias=col(R2))
        act(A("Z1", 0, 160), A("gm", 0, 160), ACT.Relu, bias=1.0, scale=-1.0)
        act(mat("TI"), A("TT", 64, 192), bias=-512.5, scale=0.5)
        act(A("Zp", 0, 160), A("Z1", 0, 160), scale=ge(14))

    def later_matrices():
        act(mat("zu"), mat("zu"), ACT.Abs, bias=col(O2))
        act(A("Zn", 0, 160), A("Z1", 0, 160), scale=lt(3))
        act(mat("Ob2"), mat("zu"), ACT.Relu, bias=1.0, scale=-1.0)
        for half in range(2):
            o = 192 + 64 * half
            act(A("TT", o, o + 20), A("TR", o, o + 20), bias=col(R40))
            act(A("TT", o + 20, o + 44), A("TR", o, o + 24), bias=col(R48))
            act(A("TT", o + 44, o + 64), A("TR", o, o + 20), bias=col(R40))
        act(mat("Ob1"), mat("Ob2"), scale=col(O1))
        for half in range(2):
            o = 192 + 64 * half
            act(A("TT", o + 20, o + 44), A("TT", o + 20, o + 44), bias=2.0 * E)
            act(A("TT", o + 44, o + 64), A("TT", o + 44, o + 64), bias=2.0 * (M - E))

    SEG = {1: (0, 20, 0, E, E), 2: (20, 44, E, M - E, 2 * E), 3: (44, 64, M - E, M, 0)}

    def rot(name, s):
        return A(name, SEG[s][4], SEG[s][4] + SEG[s][3] - SEG[s][2])

    def uplace(name, s):
        return A(name, V, V + E) if s == 1 and SCRATCH[name][1][1] == WB else A(name, SEG[s][2], SEG[s][3])

    def lplace(name, s):
        return A(name, M + SEG[s][2], M + SEG[s][3]) if s < 3 else A(name, V + E, WB)

    def width(s):
        return SEG[s][3] - SEG[s][2]

    def x_update(bank, upper, s):
        o = A(bank, 0, width(s))
        t = [(o, I, rot("XU", s)), (o, I, rot("RR", s))]
        if not upper:
            t += [(o, I, rot("DD", s)), (o, mat("nI"), rot("SS", s))]
        mm(t)

    def evac(q, out, bank, w):
        if q == "s":
            act(out, A(bank, 0, w), ACT.Copy)
        else:
            cp(out, A(bank, 0, w))

    PB = ("P0", "P1", "N0", "N1")
    deferred = []
    for k in range(RO):
        K = 4 + 2 * k
        K2 = K // 2
        last = k == RO - 1
        X, H, Mc, sc = "X%d" % k, "H%d" % k, "M%d" % k, "sc%d" % k
        Xn, Hn, Mn = "X%d" % (k + 1), "H%d" % (k + 1), "M%d" % (k + 1)

        def blk(name, kk):
            return A(name, 128 * kk, 128 * kk + 128)

        def pblk(kk):
            return A(PB[kk // 2], 128 * (kk % 2), 128 * (kk % 2) + 128)

        for kk in range(K):
            ts(blk("OH", kk), A(sc, 4, 132), float(K - 1 - kk), ALU.is_equal)
        for b in range(K2):
            mm([(A(PB[b], 0, 256), mat("Tp"), A("OH", 256 * b, 256 * b + 256))], True, False)
        scan(A("RS", 0, 128 * K), A("OH", 0, 128 * K), A("OH", 0, 128 * K), -256.0, ALU.add, ALU.min)
        mm([(A("Q1", 0, K), mat("Hb"), A("RS", 127, 128 * K, 128)), (A("Q1", 0, K), mat("Hb"), A("cm", 0, K))])
        for b in range(K2):
            mm([(A(PB[b], 0, 256), mat("B"), A("RS", 256 * b, 256 * b + 256))], False, True)
        ts(A("eb", 1, K + 1), A("Q1", 0, K), MAGIC, ALU.add, MAGIC - 2048.0, ALU.subtract)
        ts(A("eb2", 1, K + 1), A("Q1", 0, K), MAGIC, ALU.add, MAGIC - 3072.0, ALU.subtract)
        act(A("nb1", 0, K), A("eb", 0, K), bias=-1.0, scale=-1.0)
        act(A("nb2", 0, K), A("eb", 1, K + 1), scale=-2048.0)
        tt(A("t1", 0, K), A("eb", 0, K), A("eb", 1, K + 1), ALU.add)
        ts(A("e2", 0, K), A("eb", 1, K + 1), 2.0, ALU.mult)
        tt(A("d1", 0, K), A("eb2", 0, K), A("eb", 1, K + 1), ALU.subtract)
        mixed = []

        def term(q, kk, first):
            if q == "s":
                act(blk("AA", kk), pblk(kk), ACT.Relu, bias=A("nb1", kk, kk + 1))
                mixed.append((I, blk("AA", kk)))
            if first and kk < K - 1:
                if q == "s":
                    act(blk("AC", kk), pblk(kk), ACT.Relu, bias=A("nb2", kk, kk + 1), scale=1024.0)
                    mixed.append((mat("nI"), blk("AC", kk)))
                else:
                    ts(blk("AC", kk), pblk(kk), A("e2", kk, kk + 1), ALU.is_gt, -1024.0, ALU.mult)
                    mixed.append((I, blk("AC", kk)))
            if q == "v":
                ts(blk("AB", kk), pblk(kk), A("t1", kk, kk + 1), ALU.is_gt, A("d1", kk, kk + 1), ALU.mult)
                mixed.append((I, blk("AB", kk)))

        for b in range(K2):
            for kk in (2 * b, 2 * b + 1):
                term("vs"[b % 2], kk, True)
        for b in range(K2):
            for kk in (2 * b, 2 * b + 1):
                term("sv"[b % 2], kk, False)
        mm([(A("Q0", 128, 256), l, r) for l, r in mixed])
        cp(A("off", 0, 128), A("Q0", 128, 256))
        if k == 0:
            op("v", lambda e: e.tensor_copy(T.W[:, 0:V].indirect(T.off[:, 0:128]), T.M0[:, 0:V]),
               [IND("W", 0, V, "off", 0, 128)], [A("M0", 0, V)] + rows0)
            late_matrices()
        else:
            tt(IND("W", 0, V, "off", 0, 128), A(Mc, 0, V), A("C", 0, V) + tuple(x[1] for x in rowsc), ALU.add)
        for f in deferred:
            f()
        deferred = []
        act(A("sb", 0, K), A("Q1", 0, K), bias=4096.0, scale=2.0)
        act(A("hh", 0, K), A("d1", 0, K), bias=512.0, scale=-0.5)
        t0, t1, jo, bo = (64, 320, 0, 128) if last else (0, 192, 64, 0)
        for kk in range(K):
            act(A("IP", 256 * kk, 256 * kk + t1 - t0), A("TT", t0, t1), ACT.Sign, bias=A("sb", kk, kk + 1), scale=-1.0)
        for kk in range(K):
            act(blk("JJ", kk), A("IP", 256 * kk + jo, 256 * kk + jo + 128), scale=A("hh", kk, kk + 1))
        mm([(A("Q2", 0, 128), I, A("IP", 256 * kk + bo, 256 * kk + bo + 128)) for kk in range(K - 1)])
        mm([(A("Q0", 256, 384), I, mat("TI"))] + [(A("Q0", 256, 384), I, blk("JJ", kk)) for kk in range(K)])
        act(mat("y1"), A("Q0", 256, 384), bias=MAGIC, scale=0.5)
        act(mat("i16"), A("Q0", 256, 384), ACT.Copy)
        act(mat("y2"), mat("y1"), bias=2.0 * MAGIC, scale=-2.0)
        act(mat("basef"), A("Q2", 0, 128), bias=1.0 + (K - 1) / 2.0, scale=0.5)
        mm([(A("Q0", 384, 512), I, mat("i16")), (A("Q0", 384, 512), I, mat("y2"))])
        act(mat("mask"), A("Q0", 384, 512), ACT.Abs)
        if k == 0:
            later_matrices()
        mm([(A("Q1", 0, 64), band("Zp", j), A("W", j, M, 16)) for j in range(16)])
        cp(A("lu", 0, 64), A("Q1", 0, 64))
        for s in (1, 2, 3):
            a, b = SEG[s][2], SEG[s][3]
            o = A("N%d" % (s - 1), 0, b - a)
            mm([(o, mat("Nb"), A("W", M + a, M + b))] + [(o, mat("Ob1"), A("W", a, b))] * min(k, 1))
        mm([(A("Q2", 128, 192), band("Zp", j), A("W", M + j, V, 16)) for j in range(16)])
        hm = (1.0, lt(15), lt(14))[k]

        def hgather(q, out, lst, s, s_to=None):
            src = IND(H, 0, V, lst, SEG[s][0], SEG[s_to or s][1])
            if q == "s" and (k > 0 or S_INT):
                act(out, src, scale=hm)
            else:
                ts(out, src, hm, ALU.mult)

        if last:
            dma("y", A(Mn, E, M), A("W", E, M))
        hgather("v", uplace(Hn, 1), "lu", 1)
        hgather("s", uplace(Hn, 2), "lu", 2)
        hgather("s", uplace(Hn, 3), "lu", 3)
        for s in (3, 1, 2):
            act(rot("XU", s), IND(X, 0, V, "lu", SEG[s][0], SEG[s][1]), ACT.Copy)
        if not last:
            send1(prv, ep, uplace(Hn, 1), A(Hn, V - E, V), "rh%d" % k)
        for s in (1, 2, 3):
            tt(uplace("EQ", s), uplace(Hn, s), A("N%d" % (s - 1), 0, width(s)), ALU.is_equal)
        mm([(A("Q1", 64, 128), band("Z1", j), A("EQ", j, M, 16)) for j in range(16)])
        lp = A("Q2", 128, 192)
        tt(A("LOE", 0, 64), lp, A("mask", 0, 64), ALU.mult)
        tt(A("LOE", 64, 128), lp, A("mask", 64, 128), ALU.mult)
        cp(A("DI", 1, 128, 2), lp)

        def neighbours(bank, c, src, own):
            mm([(A(bank, c, c + 64), mat("Sup"), A(src, 0, 64)), (A(bank, c, c + 63), mat("Wup"), A(src, 1, 64)),
                (A(bank, c, c + 64), mat("Sdn"), A(src, 64, 128)), (A(bank, c + 1, c + 64), mat("Wdn"), A(src, 64, 127)),
                (A(bank, c, c + 64), own, A(src, 0, 64)), (A(bank, c, c + 64), own, A(src, 64, 128))])

        neighbours("Q0", 0, "LOE", mat("nI"))
        tt(A("mOE", 0, 64), A("Q1", 64, 128), A("mask", 0, 64), ALU.mult)
        tt(A("mOE", 64, 128), A("Q1", 64, 128), A("mask", 64, 128), ALU.mult)
        neighbours("Q1", 128, "mOE", I)
        cp(A("DI", 0, 128, 2), A("Q0", 0, 64))
        ts(A("F0", 1, 128, 2), A("Q1", 128, 192), 1.0, ALU.min)
        scan(mat("LS"), mat("F0"), mat("DI"), 0.0, ALU.mult, ALU.add)
        cp(A("ll", 0, 64), A("LS", 1, 128, 2))
        extra = rows0 if k == 0 else []

        def mgather(out, s, s_to=None):
            src = IND(Mc, 0, V, "ll", SEG[s][0], SEG[s_to or s][1])
            op("s", lambda e: e.activation(out[0], src[0], ACT.Copy), [out], [src] + extra)

        def m_update(bank, upper, s):
            o = A(bank, 0, width(s))
            a, b = (uplace("W", s), uplace("ML", s)) if upper else (uplace("ML", s), uplace("W", s))
            mm([(o, mat("Iz%d" % k), a), (o, mat("Sh%d" % k), b)])

        def diff(s):
            tt(rot("DD", s), IND(X, 0, V, "ll", SEG[s][0], SEG[s][1]), rot("XU", s), ALU.subtract)

        def clamp(name, s, lo):
            ts(rot(name, s), rot("DD", s), lo, ALU.max, 1.0, ALU.min)

        def sums_of(bank, c, a, w):
            if last:
                mm([(A(bank, c, c + w), band("Z1", j), A("SS", a + w * j, a + w * j + w)) for j in range(16)])
            else:
                mm([(A(bank, c, c + w), band("Z1", j), A("SS", a + j, a + 16 * w, 16)) for j in range(16)])

        def score(out, upper, s):
            c0, c1 = SEG[s][0], SEG[s][1]
            sg = A("sig", SEG[s][4] // 16, SEG[s][4] // 16 + c1 - c0)
            if upper:
                tt(out, A("basef", c0, c1), sg, ALU.subtract)
            else:
                tt(out, A("basef", 64 + c0, 64 + c1), sg, ALU.add)

        if not last:
            scn, st = "sc%d" % (k + 1), "st%d" % k
            diff(3)
            diff(1)
            mgather(uplace("ML", 1), 1)
            act(rot("SS", 3), rot("DD", 3), ACT.Sign)
            clamp("SS", 1, -1.0)
            ts(A("RR", 0, 2 * E), A("DD", 0, 2 * E), 0.0, ALU.max, 1.0, ALU.min)
            mgather(uplace("ML", 3), 3)
            m_update("N0", True, 1)
            sums_of("Q2", 192, 0, 40)
            m_update("N2", False, 3)
            ts(A("sig", 0, 40), A("Q2", 192, 232), -1.0, ALU.max, 1.0, ALU.min)
            score(A(st, 0, 20), True, 1)
            score(A(st, 24, 44), False, 3)
            send2(A(st, 0, 20), A(scn, 112, 132), A(st, 24, 44), A(scn, 4, 24), "rs%d" % k)
            evac("s", uplace(Mn, 1), "N0", E)
            evac("s", lplace(Mn, 3), "N2", E)
            send2(uplace(Mn, 1), A(Mn, V - E, V), lplace(Mn, 3), A(Mn, 0, E), "rm%d" % k)
            x_update("N1", True, 1)
            x_update("P0", False, 3)
            mgather(uplace("ML", 2), 2)
            diff(2)
            clamp("SS", 2, -1.0)
            score(A(scn, 48, 68), True, 3)
            score(A(scn, 68, 88), False, 1)
            clamp("RR", 2, 0.0)
            sums_of("Q1", 192, 2 * E, 24)
            ts(A("sig", 40, 64), A("Q1", 192, 216), -1.0, ALU.max, 1.0, ALU.min)
            score(A(scn, 24, 48), True, 2)
            score(A(scn, 88, 112), False, 2)
            hgather("s", lplace(Hn, 3), "ll", 3)
            evac("s", uplace(Xn, 1), "N1", E)
            evac("s", lplace(Xn, 3), "P0", E)
            send1(nxt, en, lplace(Hn, 3), A(Hn, 0, E), "rh%d" % k)
            send2(uplace(Xn, 1), A(Xn, V - E, V), lplace(Xn, 3), A(Xn, 0, E), "rx%d" % k)
            for bank, up, s in (("N0", True, 2), ("N2", True, 3), ("N1", False, 1), ("P1", False, 2)):
                m_update(bank, up, s)
            for bank, up, s in (("N0", True, 2), ("N2", True, 3), ("N1", False, 1), ("P1", False, 2)):
                evac("s", uplace(Mn, s) if up else lplace(Mn, s), bank, width(s))
            if k == 0 and not S_INT:
                hgather("v", A(Hn, M, V - E), "ll", 1, 2)
            arrive("rs%d" % k, n_half, A(scn, 4, 24), A(scn, 112, 132))
            arrive("rm%d" % k, n_half, A(Mn, 0, E), A(Mn, V - E, V))
            arrive("rx%d" % k, n_half, A(Xn, 0, E), A(Xn, V - E, V))
            arrive("rh%d" % k, n_full, A(Hn, 0, E), A(Hn, V - E, V))

            def rest(k=k, H=H, Hn=Hn, Xn=Xn, hm=hm):
                four = (("N0", True, 2), ("N2", True, 3), ("N1", False, 1), ("P0", False, 2))
                for bank, up, s in four:
                    x_update(bank, up, s)
                if k > 0 or S_INT:
                    act(A(Hn, M, V - E), IND(H, 0, V, "ll", 0, 44), scale=hm)
                for bank, up, s in four:
                    evac("s", uplace(Xn, s) if up else lplace(Xn, s), bank, width(s))
            deferred.append(rest)
        else:
            def names(bank, c, src, a, w):
                mm([(A(bank, c, c + w), band("Zn", j), A(src, a + w * j, a + w * j + w)) for j in range(16)])

            def out(q, name, a, b, src):
                dma(q, hbm(T[name][:, a:b], name, a, b), src)

            names("Q0", 64, "W", 0, 20)
            mgather(lplace(Mn, 3), 3)
            act(A("stf", 20, 40), A("Q0", 64, 84), ACT.Copy)
            diff(3)
            ts(A("LT", 0, E), rot("DD", 3), 0.0, ALU.is_lt)
            diff(1)
            clamp("RR", 1, 0.0)
            ts(A("SS", 0, 2 * E), A("DD", 0, 2 * E), -1.0, ALU.max, 1.0, ALU.min)
            o = A("P0", 0, E)
            mm([(o, I, rot("XU", 3)), (o, I, rot("DD", 3)), (o, I, A("LT", 0, E))])
            evac("s", lplace(Xn, 3), "P0", E)
            send1(nxt, en, lplace(Xn, 3), A(Xn, 0, E), "rx%d" % k)
            names("Q0", 84, Mn, V + E, 20)
            x_update("N1", True, 1)
            evac("v", uplace(Xn, 1), "N1", E)
            send1(prv, ep, uplace(Xn, 1), A(Xn, V - E, V), "rx%d" % k)
            act(A("stf", 60, 80), A("Q0", 84, 104), ACT.Copy)
            mgather(A(Mn, M, V - E), 1, 2)
            sums_of("Q2", 192, 0, 20)
            sums_of("Q2", 212, E, 20)
            clamp("RR", 3, 0.0)
            diff(2)
            ts(A("sig", 0, 40), A("Q2", 192, 232), -1.0, ALU.max, 1.0, ALU.min)
            score(A("stf", 0, 20), True, 1)
            score(A("stf", 40, 60), False, 3)
            send2(A("stf", 0, 40), A("lf", 40, 80), A("stf", 40, 80), A("lf", 0, 40), "rs%d" % k)
            clamp("SS", 2, -1.0)
            clamp("RR", 2, 0.0)
            x_update("N0", True, 3)
            x_update("N2", False, 1)
            evac("s", uplace(Xn, 3), "N0", E)
            evac("s", lplace(Xn, 1), "N2", E)
            out("y", "yx", M - E, M + E, A(Xn, M - E, M + E))
            x_update("N1", True, 2)
            x_update("P0", False, 2)
            sums_of("Q1", 192, 2 * E, 24)
            names("Q0", 128, Mn, E, 88)
            score(A("fo", 44, 64), True, 3)
            score(A("fo", 64, 84), False, 1)
            out("y", "ys", M - E, M, A("fo", 44, 64))
            out("y", "ys", M, M + E, A("fo", 64, 84))
            evac("s", uplace(Xn, 2), "N1", width(2))
            evac("v", lplace(Xn, 2), "P0", width(2))
            out("y", "yx", E, M - E, uplace(Xn, 2))
            out("y", "yx", M + E, V - E, lplace(Xn, 2))
            ts(A("sig", 40, 64), A("Q1", 192, 216), -1.0, ALU.max, 1.0, ALU.min)
            score(A("fo", 20, 44), True, 2)
            score(A("fo", 84, 108), False, 2)
            act(A("fn", 0, 88), A("Q0", 128, 216), ACT.Copy)
            out("y", "ys", E, M - E, A("fo", 20, 44))
            out("y", "ys", M + E, V - E, A("fo", 84, 108))
            out("s", "yn", E, V - E, A("fn", 0, 88))
            arrive("rx%d" % k, n_full, A(Xn, 0, E), A(Xn, V - E, V))
            arrive("rs%d" % k, n_half, A("lf", 0, 80))
            out("y", "yx", V - E, V, A(Xn, V - E, V))
            out("s", "yx", 0, E, A(Xn, 0, E))
            out("y", "ys", V - E, V, A("lf", 40, 60))
            out("s", "ys", 0, E, A("lf", 0, 20))
            out("y", "yn", V - E, V, A("lf", 60, 80))
            out("s", "yn", 0, E, A("lf", 20, 40))
    _emit(g, T, ops)
